import numpy as np
import ml_dtypes


def mxq(x, axis, fmt="e4m3"):
    dtype, down = {"e4m3": (ml_dtypes.float8_e4m3fn, 7), "e5m2": (ml_dtypes.float8_e5m2, 14)}[fmt]
    v = np.moveaxis(np.asarray(x, np.float32).astype(ml_dtypes.bfloat16).astype(np.float64), axis, -1)
    blocks = v.reshape(v.shape[:-1] + (-1, 32))
    amax = np.abs(blocks).max(-1, keepdims=True)
    byte = np.maximum(np.where(amax > 0, np.frexp(amax)[1] - 1 + 127, 0) - down, 1)
    scale = np.exp2(byte - 127.0)
    codes = (blocks / scale).astype(np.float32).astype(dtype).astype(np.float64)
    return np.moveaxis((codes * scale).reshape(v.shape), -1, axis)


WIDE = False


def mx_kscale(k):
    if not WIDE:
        return np.ones(k)
    levels = np.array([30, -30])
    if k % 512:
        return np.exp2(np.random.permutation(np.resize(levels, k // 32))).repeat(32)
    a = np.empty((k // 512, 16))
    for p in range(k // 512):
        a[p, :8] = np.random.permutation(np.resize(levels, 8))
        for g in range(8):
            far = levels[np.abs(levels - a[p, g]) >= 10]
            a[p, g + 8] = far[np.random.randint(len(far))]
    return np.exp2(a.ravel()).repeat(32)


def f64(x):
    return np.asarray(x).astype(np.float64)


def striped(idx):
    return np.tile(np.asarray(idx).reshape(-1, 16).T, (8, 1)).astype(np.uint16)


def unstriped(offs):
    return offs[:16].T.reshape(-1).astype(np.int64)


E2M1 = np.array([0.0, 0.5, 1.0, 1.5, 2.0, 3.0, 4.0, 6.0, -0.0, -0.5, -1.0, -1.5, -2.0, -3.0, -4.0, -6.0])


def pack_weight(w, fmt):
    k, n = w.shape
    w = f64(np.asarray(w, np.float32).astype(ml_dtypes.bfloat16)).reshape(k // 32, 32, n)
    amax = np.abs(w).max(1)
    if fmt in ("e4m3", "e5m2"):
        byte = np.frexp(amax)[1] - 1 + 127 - (7 if fmt == "e4m3" else 14)
    else:
        mant, ex = np.frexp(amax / 6.0)
        byte = np.where(mant > 0.5, ex, ex - 1) + 127
    byte = np.clip(np.where(amax > 0, byte, 1), 1, 254)
    scaled = (w * np.exp2(127.0 - byte)[:, None, :]).reshape(k, n).astype(np.float32)
    by_word = np.ascontiguousarray(scaled.reshape(k // 512, 128, 4, n).transpose(0, 1, 3, 2))
    if fmt in ("e4m3", "e5m2"):
        words = by_word.astype(ml_dtypes.float8_e4m3fn if fmt == "e4m3" else ml_dtypes.float8_e5m2).view(np.uint8)
    else:
        c = by_word.astype(ml_dtypes.float4_e2m1fn).view(np.uint8) & 0xF
        words = (c[..., 0::2] | (c[..., 1::2] << 4)).reshape(k // 512, 128, 2 * n)
    return np.ascontiguousarray(words), np.ascontiguousarray(byte.astype(np.uint8).reshape(k // 512, 16, n))


def unpack_weight(words, scales, fmt):
    g, _, n = scales.shape
    words = np.ascontiguousarray(words).reshape(g, 128, n, -1)
    if fmt in ("e4m3", "e5m2"):
        vals = words.view(ml_dtypes.float8_e4m3fn if fmt == "e4m3" else ml_dtypes.float8_e5m2).astype(np.float64)
    else:
        nib = np.empty((g, 128, n, 4), np.uint8)
        nib[..., 0::2] = words & 0xF
        nib[..., 1::2] = words >> 4
        vals = E2M1[nib]
    vals = vals * np.repeat(np.exp2(scales.astype(np.float64) - 127.0), 8, axis=1)[..., None]
    return vals.transpose(0, 1, 3, 2).reshape(g * 512, n)


K, T, J, R, C, O, N, E = 512, 1024, 256, 512, 512, 256, 256, 1024


def setup_inputs():
    n = np.random.standard_normal
    idx = np.random.permutation(T)[:J]
    idx2 = np.random.permutation(C)[:J]
    idx3 = np.random.permutation(C)[:J]
    idx4 = np.random.permutation(C)[:O]
    idx5 = np.random.permutation(T)[:O]
    idx6 = np.random.permutation(E)[:O]
    fk = mx_kscale(K)
    fr = mx_kscale(R)
    xtp = pack_weight(n((K, T)) / fk[:, None], "e4m3")
    wp = pack_weight(n((K, R)) * 1 / np.sqrt(K) * fk[:, None] * fr, "e2m1")
    wbp = pack_weight(n((R, N)) * 1 / np.sqrt(R) / fr[:, None], "e5m2")
    wsp = pack_weight(n((K, N)) * 1 / np.sqrt(K) * fk[:, None], "e5m2")
    return {
        "xt_words": xtp[0],
        "xt_scales": xtp[1],
        "w_words": wp[0],
        "w_scales": wp[1],
        "wb_words": wbp[0],
        "wb_scales": wbp[1],
        "ws_words": wsp[0],
        "ws_scales": wsp[1],
        "tz": (n((N, E))).astype(np.float32),
        "offs": striped(idx),
        "offs2": striped(idx2),
        "offs3": striped(idx3),
        "offs4": striped(idx4),
        "offs5": striped(idx5),
        "offs6": striped(idx6),
    }


def reference(xt_words, xt_scales, w_words, w_scales, wb_words, wb_scales, ws_words, ws_scales, tz, offs, offs2, offs3, offs4, offs5, offs6):
    idx = unstriped(offs)
    idx2 = unstriped(offs2)
    idx3 = unstriped(offs3)
    idx4 = unstriped(offs4)
    idx5 = unstriped(offs5)
    idx6 = unstriped(offs6)
    xtu = unpack_weight(xt_words, xt_scales, "e4m3")
    wu = unpack_weight(w_words, w_scales, "e2m1")
    wbu = unpack_weight(wb_words, wb_scales, "e5m2")
    wsu = unpack_weight(ws_words, ws_scales, "e5m2")
    xtidxg = xtu[:, idx]
    a = wu.T @ xtidxg
    pw = np.zeros((R, C))
    pw[:, idx2] = a
    pv = np.zeros((R, C))
    pv[:, idx3] = a
    pg = pw + pv
    hid = np.maximum(pg[:, idx4], 0.0)
    hidq = mxq(hid, 0, "e4m3")
    xtidx5g = xtu[:, idx5]
    p = wbu.T @ hidq + wsu.T @ xtidx5g
    y = p + f64(tz)[:, idx6]
    return y

@@ -1,0 +1,159 @@
+from contextlib import ExitStack
+
+import concourse.mybir as mybir
+
+K, T, J, R, C, O, N, E = 512, 1024, 256, 512, 512, 256, 256, 1024
+FLOPS = 2 * K * R * J + 2 * R * N * O + 2 * K * N * O
+
+F32 = mybir.dt.float32
+BF16 = mybir.dt.bfloat16
+I32 = mybir.dt.int32
+U32 = mybir.dt.uint32
+U16 = mybir.dt.uint16
+U8 = mybir.dt.uint8
+E4M3 = mybir.dt.float8_e4m3fn_x4
+E5M2 = mybir.dt.float8_e5m2_x4
+E2M1 = mybir.dt.float4_e2m1fn_x4
+ALU = mybir.AluOpType
+COPY = mybir.ActivationFunctionType.Copy
+
+P = 128
+PACK = 4
+
+
+def tile_list_postedtwice_solo_further_tabled_kernel(
+    tc, xt_words, xt_scales, w_words, w_scales, wb_words, wb_scales, ws_words, ws_scales, tz,
+    offs, offs2, offs3, offs4, offs5, offs6, out,
+):
+    nc = tc.nc
+    with ExitStack() as ctx:
+        keep = ctx.enter_context(tc.tile_pool(name="keep", bufs=1))
+        psum = ctx.enter_context(tc.psum_pool(name="psum", bufs=1))
+
+        def sb(shape, dtype, name):
+            return keep.tile(shape, dtype, name=name, align_bytes=64)
+
+        def load_list(src, name):
+            t = sb([P, 16], U16, name)
+            nc.sync.dma_start(t[:], src)
+            return t
+
+        def load_words(src2d, width_bytes, name):
+            t = sb([P, width_bytes // 4], I32, name)
+            nc.sync.dma_start(t[:], src2d.bitcast(I32))
+            return t
+
+        def load_scale_rows(queue, plane, src, q):
+            queue.dma_start(plane[32 * q : 32 * q + 4, :].bitcast(I32), src[0, 4 * q : 4 * q + 4, :].bitcast(I32))
+
+        xt_s = sb([P, T], U8, "xt_s")
+        nc.vector.memset(xt_s[:].bitcast(I32), 0)
+        w_s = sb([P, R], U8, "w_s")
+        nc.gpsimd.memset(w_s[:].bitcast(I32), 0)
+        ws_s = sb([P, N], U8, "ws_s")
+        wb_s = sb([P, N], U8, "wb_s")
+
+        l1 = load_list(offs, "l1")
+        l2 = load_list(offs2, "l2")
+        l3 = load_list(offs3, "l3")
+        for q in range(4):
+            load_scale_rows(nc.sync, xt_s, xt_scales, q)
+        xt_w = load_words(xt_words[0].rearrange("p c r -> p (c r)"), 4 * T, "xt_w")
+        w_w = load_words(w_words[0], 2 * R, "w_w")
+        for q in range(4):
+            load_scale_rows(nc.sync, w_s, w_scales, q)
+        l5 = load_list(offs5, "l5")
+        l4 = load_list(offs4, "l4")
+        ws_w = load_words(ws_words[0].rearrange("p c r -> p (c r)"), 4 * N, "ws_w")
+        wb_w = load_words(wb_words[0].rearrange("p c r -> p (c r)"), 4 * N, "wb_w")
+        l6 = load_list(offs6, "l6")
+        nc.gpsimd.memset(ws_s[:].bitcast(I32), 0)
+        nc.gpsimd.memset(wb_s[:].bitcast(I32), 0)
+        for q in range(4):
+            load_scale_rows(nc.sync, ws_s, ws_scales, q)
+        for q in range(4):
+            load_scale_rows(nc.sync, wb_s, wb_scales, q)
+        tz_t = []
+        for c in range(N // P):
+            t = sb([P, E], F32, "tz%d" % c)
+            nc.sync.dma_start(t[:], tz[c * P : (c + 1) * P, :])
+            tz_t.append(t)
+
+        pw = [sb([P, C], F32, "pw%d" % t) for t in range(PACK)]
+        pv = [sb([P, C], F32, "pv%d" % t) for t in range(PACK)]
+        for t in range(PACK):
+            nc.vector.memset(pw[t][:], 0.0)
+            nc.gpsimd.memset(pv[t][:], 0.0)
+
+        def gather_tokens(lst, name):
+            gs = sb([P, J], U8, name + "_s")
+            nc.vector.tensor_copy(gs[:], xt_s[:].indirect(lst[:]))
+            gw = sb([P, J], U32, name + "_w")
+            nc.vector.tensor_copy(gw[:], xt_w[:].bitcast(U32).indirect(lst[:]))
+            return gw, gs
+
+        x1_w, x1_s = gather_tokens(l1, "x1")
+
+        a_ps = []
+        for t in range(PACK):
+            wt_w = sb([P, 2 * P], U8, "wt_w%d" % t)
+            nc.scalar.copy(wt_w[:].bitcast(U16), w_w[:].bitcast(U16)[:, t : R : PACK])
+            wt_s = sb([P, P], U8, "wt_s%d" % t)
+            nc.vector.tensor_copy(wt_s[:], w_s[:, t : R : PACK])
+            acc = psum.tile([P, J], F32, name="a_ps%d" % t)
+            nc.tensor.matmul_mx(acc[:], lhsT=wt_w[:].bitcast(E2M1), lhsT_scale=wt_s[:],
+                                rhs=x1_w[:].bitcast(E4M3), rhs_scale=x1_s[:], start=True, stop=True)
+            a_ps.append(acc)
+
+        x5_w, x5_s = gather_tokens(l5, "x5")
+        H = O // 2
+        p_ps = []
+        for h in range(2):
+            acc = psum.tile([P, N // P, H], F32, name="p_ps%d" % h)
+            reads = slice(h * H, (h + 1) * H)
+            for c in range(N // P):
+                cols = slice(c * P, (c + 1) * P)
+                nc.tensor.matmul_mx(acc[:, c, :], lhsT=ws_w[:, cols].bitcast(E5M2), lhsT_scale=ws_s[:, cols],
+                                    rhs=x5_w[:, reads].bitcast(E4M3), rhs_scale=x5_s[:, reads], start=(c == 0), stop=False)
+            p_ps.append(acc)
+
+        a_sb = [sb([P, J], F32, "a_sb%d" % t) for t in range(PACK)]
+        nc.scalar.copy(a_sb[0][:], a_ps[0][:])
+        nc.vector.tensor_copy(a_sb[1][:], a_ps[1][:])
+        picked = sb([P, PACK, O], F32, "picked")
+        for t in range(PACK):
+            nc.vector.tensor_copy(pw[t][:].indirect(l2[:]), a_sb[t][:])
+            nc.scalar.activation(pv[t][:].indirect(l3[:]), a_sb[t][:], COPY)
+            if t + 2 < PACK:
+                nc.scalar.copy(a_sb[t + 2][:], a_ps[t + 2][:])
+        for t in range(PACK):
+            board = keep.tile([P, C], F32, name="pg%d" % t, tag="pg%d" % t, align_bytes=64)
+            nc.vector.tensor_tensor(board[:], pw[t][:], pv[t][:], ALU.add)
+            if t < PACK - 1:
+                nc.scalar.activation(picked[:, t, :], board[:].indirect(l4[:]), COPY)
+            else:
+                nc.vector.tensor_copy(picked[:, t, :H], board[:].indirect(l4[:, : H // 16]))
+                nc.scalar.activation(picked[:, t, H:], board[:].indirect(l4[:, H // 16 :]), COPY)
+
+        tzg = keep.tile([P, N // P, O], F32, name="tzg", tag="pg%d" % (PACK - 1), align_bytes=64)
+        for c in range(N // P):
+            nc.scalar.activation(tzg[:, c, :], tz_t[c][:].indirect(l6[:]), COPY)
+
+        hid, hid_w, hid_s = [], [], []
+        for h in range(2):
+            hid.append(sb([P, H, PACK], BF16, "hid%d" % h))
+            nc.vector.tensor_scalar_max(hid[h][:], picked[:, :, h * H : (h + 1) * H].rearrange("p t o -> p o t"), 0.0)
+        for h in range(2):
+            hid_w.append(sb([P, H], U32, "hid_w%d" % h))
+            hid_s.append(sb([P, H], U8, "hid_s%d" % h))
+            nc.vector.quantize_mx(hid_w[h][:].bitcast(E4M3), hid_s[h][:], hid[h][:].rearrange("p o t -> p (o t)"))
+            for c in range(N // P):
+                cols = slice(c * P, (c + 1) * P)
+                nc.tensor.matmul_mx(p_ps[h][:, c, :], lhsT=wb_w[:, cols].bitcast(E5M2), lhsT_scale=wb_s[:, cols],
+                                    rhs=hid_w[h][:].bitcast(E4M3), rhs_scale=hid_s[h][:], start=False, stop=(c == N // P - 1))
+        out_rows = out.rearrange("(c p) o -> p c o", p=P)
+        for h in range(2):
+            reads = slice(h * H, (h + 1) * H)
+            y = sb([P, N // P, H], F32, "y%d" % h)
+            nc.vector.tensor_tensor(y[:], p_ps[h][:], tzg[:, :, reads], ALU.add)
+            nc.sync.dma_start(out_rows[:, :, reads], y[:])

@@ -38,61 +38,65 @@ def tile_list_postedtwice_solo_further_tabled_kernel(
             nc.sync.dma_start(t[:], src)
             return t
 
-        def load_words(src2d, width_bytes, name):
+        def load_words(queue, src2d, width_bytes, name):
             t = sb([P, width_bytes // 4], I32, name)
-            nc.sync.dma_start(t[:], src2d.bitcast(I32))
+            queue.dma_start(t[:], src2d.bitcast(I32))
             return t
 
-        def load_scale_rows(queue, plane, src, q):
-            queue.dma_start(plane[32 * q : 32 * q + 4, :].bitcast(I32), src[0, 4 * q : 4 * q + 4, :].bitcast(I32))
+        def load_scale_rows(plane, src, q):
+            nc.sync.dma_start(plane[32 * q : 32 * q + 4, :].bitcast(I32), src[0, 4 * q : 4 * q + 4, :].bitcast(I32))
+
+        def load_token_scales(queue, q):
+            rows = xt_scales[0, 4 * q : 4 * q + 4, :].bitcast(I32)
+            queue.dma_start(xt_s[32 * q : 32 * (q + 1), :].bitcast(I32), rows.unsqueeze(0).to_broadcast([8, 4, T // 4]))
 
         xt_s = sb([P, T], U8, "xt_s")
-        nc.vector.memset(xt_s[:].bitcast(I32), 0)
-        w_s = sb([P, R], U8, "w_s")
-        nc.gpsimd.memset(w_s[:].bitcast(I32), 0)
+        w_s = keep.tile([P, R], U8, name="w_s", tag="w_s", align_bytes=64)
         ws_s = sb([P, N], U8, "ws_s")
         wb_s = sb([P, N], U8, "wb_s")
+        for plane in (w_s, ws_s, wb_s):
+            nc.gpsimd.memset(plane[:].bitcast(I32), 0)
 
         l1 = load_list(offs, "l1")
+        l5 = load_list(offs5, "l5")
+        for q in range(3):
+            load_token_scales(nc.scalar, q)
+        load_token_scales(nc.sync, 3)
+        xt_w = load_words(nc.sync, xt_words[0].rearrange("p c r -> p (c r)"), 4 * T, "xt_w")
+        w_w = load_words(nc.scalar, w_words[0], 2 * R, "w_w")
+        for q in range(4):
+            load_scale_rows(w_s, w_scales, q)
         l2 = load_list(offs2, "l2")
         l3 = load_list(offs3, "l3")
+        ws_w = load_words(nc.sync, ws_words[0].rearrange("p c r -> p (c r)"), 4 * N, "ws_w")
+        wb_w = load_words(nc.sync, wb_words[0].rearrange("p c r -> p (c r)"), 4 * N, "wb_w")
         for q in range(4):
-            load_scale_rows(nc.sync, xt_s, xt_scales, q)
-        xt_w = load_words(xt_words[0].rearrange("p c r -> p (c r)"), 4 * T, "xt_w")
-        w_w = load_words(w_words[0], 2 * R, "w_w")
-        for q in range(4):
-            load_scale_rows(nc.sync, w_s, w_scales, q)
-        l5 = load_list(offs5, "l5")
+            load_scale_rows(ws_s, ws_scales, q)
         l4 = load_list(offs4, "l4")
-        ws_w = load_words(ws_words[0].rearrange("p c r -> p (c r)"), 4 * N, "ws_w")
-        wb_w = load_words(wb_words[0].rearrange("p c r -> p (c r)"), 4 * N, "wb_w")
+        for q in range(4):
+            load_scale_rows(wb_s, wb_scales, q)
         l6 = load_list(offs6, "l6")
-        nc.gpsimd.memset(ws_s[:].bitcast(I32), 0)
-        nc.gpsimd.memset(wb_s[:].bitcast(I32), 0)
-        for q in range(4):
-            load_scale_rows(nc.sync, ws_s, ws_scales, q)
-        for q in range(4):
-            load_scale_rows(nc.sync, wb_s, wb_scales, q)
         tz_t = []
         for c in range(N // P):
             t = sb([P, E], F32, "tz%d" % c)
             nc.sync.dma_start(t[:], tz[c * P : (c + 1) * P, :])
             tz_t.append(t)
 
-        pw = [sb([P, C], F32, "pw%d" % t) for t in range(PACK)]
-        pv = [sb([P, C], F32, "pv%d" % t) for t in range(PACK)]
-        for t in range(PACK):
+        BOARDS = 3
+        pw = [sb([P, C], F32, "pw%d" % t) for t in range(BOARDS)]
+        pv = [sb([P, C], F32, "pv%d" % t) for t in range(BOARDS)]
+        for t in range(BOARDS):
             nc.vector.memset(pw[t][:], 0.0)
-            nc.gpsimd.memset(pv[t][:], 0.0)
+            nc.vector.memset(pv[t][:], 0.0)
 
-        def gather_tokens(lst, name):
+        def gather_tokens(lst, name, words_tag):
             gs = sb([P, J], U8, name + "_s")
             nc.vector.tensor_copy(gs[:], xt_s[:].indirect(lst[:]))
-            gw = sb([P, J], U32, name + "_w")
+            gw = keep.tile([P, J], U32, name=name + "_w", tag=words_tag, align_bytes=64)
             nc.vector.tensor_copy(gw[:], xt_w[:].bitcast(U32).indirect(lst[:]))
             return gw, gs
 
-        x1_w, x1_s = gather_tokens(l1, "x1")
+        x1_w, x1_s = gather_tokens(l1, "x1", "x1_w")
 
         a_ps = []
         for t in range(PACK):
@@ -105,7 +109,7 @@ def tile_list_postedtwice_solo_further_tabled_kernel(
                                 rhs=x1_w[:].bitcast(E4M3), rhs_scale=x1_s[:], start=True, stop=True)
             a_ps.append(acc)
 
-        x5_w, x5_s = gather_tokens(l5, "x5")
+        x5_w, x5_s = gather_tokens(l5, "x5", "w_s")
         H = O // 2
         p_ps = []
         for h in range(2):
@@ -118,31 +122,48 @@ def tile_list_postedtwice_solo_further_tabled_kernel(
             p_ps.append(acc)
 
         a_sb = [sb([P, J], F32, "a_sb%d" % t) for t in range(PACK)]
-        nc.scalar.copy(a_sb[0][:], a_ps[0][:])
-        nc.vector.tensor_copy(a_sb[1][:], a_ps[1][:])
+        boards = []
         picked = sb([P, PACK, O], F32, "picked")
-        for t in range(PACK):
-            nc.vector.tensor_copy(pw[t][:].indirect(l2[:]), a_sb[t][:])
-            nc.scalar.activation(pv[t][:].indirect(l3[:]), a_sb[t][:], COPY)
-            if t + 2 < PACK:
-                nc.scalar.copy(a_sb[t + 2][:], a_ps[t + 2][:])
-        for t in range(PACK):
+
+        def post(t):
+            nc.vector.tensor_copy(pw[t % BOARDS][:].indirect(l2[:]), a_sb[t][:])
+            nc.scalar.activation(pv[t % BOARDS][:].indirect(l3[:]), a_sb[t][:], COPY)
+
+        def add(t):
             board = keep.tile([P, C], F32, name="pg%d" % t, tag="pg%d" % t, align_bytes=64)
-            nc.vector.tensor_tensor(board[:], pw[t][:], pv[t][:], ALU.add)
+            nc.vector.tensor_tensor(board[:], pw[t % BOARDS][:], pv[t % BOARDS][:], ALU.add)
+            return board
+
+        def read(t, board):
             if t < PACK - 1:
                 nc.scalar.activation(picked[:, t, :], board[:].indirect(l4[:]), COPY)
             else:
                 nc.vector.tensor_copy(picked[:, t, :H], board[:].indirect(l4[:, : H // 16]))
                 nc.scalar.activation(picked[:, t, H:], board[:].indirect(l4[:, H // 16 :]), COPY)
 
-        tzg = keep.tile([P, N // P, O], F32, name="tzg", tag="pg%d" % (PACK - 1), align_bytes=64)
-        for c in range(N // P):
-            nc.scalar.activation(tzg[:, c, :], tz_t[c][:].indirect(l6[:]), COPY)
+        nc.scalar.copy(a_sb[0][:], a_ps[0][:])
+        for t in range(PACK):
+            if t + 1 < PACK:
+                nc.scalar.copy(a_sb[t + 1][:], a_ps[t + 1][:])
+            post(t)
+            if t >= 2:
+                read(t - 2, boards[t - 2])
+            if t >= 1:
+                boards.append(add(t - 1))
+        boards.append(add(PACK - 1))
+        for t in range(PACK - 2, PACK):
+            read(t, boards[t])
+
+        tzg = keep.tile([P, 2, N // P, H], F32, name="tzg", tag="pg%d" % (PACK - 1), align_bytes=64)
+        for h in range(2):
+            for c in range(N // P):
+                nc.scalar.activation(tzg[:, h, c, :], tz_t[c][:].indirect(l6[:, h * H // 16 : (h + 1) * H // 16]), COPY)
 
         hid, hid_w, hid_s = [], [], []
         for h in range(2):
             hid.append(sb([P, H, PACK], BF16, "hid%d" % h))
-            nc.vector.tensor_scalar_max(hid[h][:], picked[:, :, h * H : (h + 1) * H].rearrange("p t o -> p o t"), 0.0)
+            nc.vector.tensor_scalar_max(hid[h][:].rearrange("p (g i) t -> p g t i", i=4),
+                                        picked[:, :, h * H : (h + 1) * H].rearrange("p t (g i) -> p g t i", i=4), 0.0)
         for h in range(2):
             hid_w.append(sb([P, H], U32, "hid_w%d" % h))
             hid_s.append(sb([P, H], U8, "hid_s%d" % h))
@@ -155,5 +176,5 @@ def tile_list_postedtwice_solo_further_tabled_kernel(
         for h in range(2):
             reads = slice(h * H, (h + 1) * H)
             y = sb([P, N // P, H], F32, "y%d" % h)
-            nc.vector.tensor_tensor(y[:], p_ps[h][:], tzg[:, :, reads], ALU.add)
+            nc.vector.tensor_tensor(y[:], p_ps[h][:], tzg[:, h], ALU.add)
             nc.sync.dma_start(out_rows[:, :, reads], y[:])

@@ -99,13 +99,17 @@ def tile_list_postedtwice_solo_further_tabled_kernel(
         x1_w, x1_s = gather_tokens(l1, "x1", "x1_w")
 
         a_ps = []
+        wt_s0 = sb([P, P], U8, "wt_s0")
+        wt_s1 = sb([P, PACK - 1, P], U8, "wt_s1")
+        dealt = w_s[:].rearrange("p (m t) -> p t m", t=PACK)
+        nc.vector.tensor_copy(wt_s0[:], dealt[:, 0, :])
+        nc.vector.tensor_copy(wt_s1[:], dealt[:, 1:, :])
         for t in range(PACK):
             wt_w = sb([P, 2 * P], U8, "wt_w%d" % t)
             nc.scalar.copy(wt_w[:].bitcast(U16), w_w[:].bitcast(U16)[:, t : R : PACK])
-            wt_s = sb([P, P], U8, "wt_s%d" % t)
-            nc.vector.tensor_copy(wt_s[:], w_s[:, t : R : PACK])
+            wt_s = wt_s0[:] if t == 0 else wt_s1[:, t - 1, :]
             acc = psum.tile([P, J], F32, name="a_ps%d" % t)
-            nc.tensor.matmul_mx(acc[:], lhsT=wt_w[:].bitcast(E2M1), lhsT_scale=wt_s[:],
+            nc.tensor.matmul_mx(acc[:], lhsT=wt_w[:].bitcast(E2M1), lhsT_scale=wt_s,
                                 rhs=x1_w[:].bitcast(E4M3), rhs_scale=x1_s[:], start=True, stop=True)
             a_ps.append(acc)
 
@@ -130,31 +134,34 @@ def tile_list_postedtwice_solo_further_tabled_kernel(
             nc.scalar.activation(pv[t % BOARDS][:].indirect(l3[:]), a_sb[t][:], COPY)
 
         def add(t):
-            board = keep.tile([P, C], F32, name="pg%d" % t, tag="pg%d" % t, align_bytes=64)
-            nc.vector.tensor_tensor(board[:], pw[t % BOARDS][:], pv[t % BOARDS][:], ALU.add)
+            board = keep.tile([P, C], F32, name="pg%d" % t, tag="pg%d" % (t % BOARDS), align_bytes=64)
+            (nc.gpsimd if t < PACK - 1 else nc.vector).tensor_tensor(board[:], pw[t % BOARDS][:], pv[t % BOARDS][:], ALU.add)
             return board
 
         def read(t, board):
-            if t < PACK - 1:
+            if t == 0:
+                nc.vector.tensor_copy(picked[:, t, :], board[:].indirect(l4[:]))
+            elif t < PACK - 1:
                 nc.scalar.activation(picked[:, t, :], board[:].indirect(l4[:]), COPY)
             else:
-                nc.vector.tensor_copy(picked[:, t, :H], board[:].indirect(l4[:, : H // 16]))
+                nc.scalar.activation(picked[:, t, :H], board[:].indirect(l4[:, : H // 16]), COPY)
                 nc.scalar.activation(picked[:, t, H:], board[:].indirect(l4[:, H // 16 :]), COPY)
 
         nc.scalar.copy(a_sb[0][:], a_ps[0][:])
         for t in range(PACK):
-            if t + 1 < PACK:
-                nc.scalar.copy(a_sb[t + 1][:], a_ps[t + 1][:])
             post(t)
-            if t >= 2:
-                read(t - 2, boards[t - 2])
-            if t >= 1:
-                boards.append(add(t - 1))
+            if t == 0:
+                nc.vector.tensor_copy(a_sb[1][:], a_ps[1][:])
+            if t + 2 < PACK:
+                nc.scalar.copy(a_sb[t + 2][:], a_ps[t + 2][:])
+            if t < PACK - 1:
+                boards.append(add(t))
+        read(0, boards[0])
         boards.append(add(PACK - 1))
-        for t in range(PACK - 2, PACK):
+        for t in range(1, PACK):
             read(t, boards[t])
 
-        tzg = keep.tile([P, 2, N // P, H], F32, name="tzg", tag="pg%d" % (PACK - 1), align_bytes=64)
+        tzg = keep.tile([P, 2, N // P, H], F32, name="tzg", tag="pg0", align_bytes=64)
         for h in range(2):
             for c in range(N // P):
                 nc.scalar.activation(tzg[:, h, c, :], tz_t[c][:].indirect(l6[:, h * H // 16 : (h + 1) * H // 16]), COPY)

@@ -43,8 +43,8 @@ def tile_list_postedtwice_solo_further_tabled_kernel(
             queue.dma_start(t[:], src2d.bitcast(I32))
             return t
 
-        def load_scale_rows(plane, src, q):
-            nc.sync.dma_start(plane[32 * q : 32 * q + 4, :].bitcast(I32), src[0, 4 * q : 4 * q + 4, :].bitcast(I32))
+        def load_scale_rows(plane, src, q, queue=nc.sync):
+            queue.dma_start(plane[32 * q : 32 * q + 4, :].bitcast(I32), src[0, 4 * q : 4 * q + 4, :].bitcast(I32))
 
         def load_token_scales(queue, q):
             rows = xt_scales[0, 4 * q : 4 * q + 4, :].bitcast(I32)
@@ -65,7 +65,7 @@ def tile_list_postedtwice_solo_further_tabled_kernel(
         xt_w = load_words(nc.sync, xt_words[0].rearrange("p c r -> p (c r)"), 4 * T, "xt_w")
         w_w = load_words(nc.scalar, w_words[0], 2 * R, "w_w")
         for q in range(4):
-            load_scale_rows(w_s, w_scales, q)
+            load_scale_rows(w_s, w_scales, q, nc.sync if q % 2 == 0 else nc.scalar)
         l2 = load_list(offs2, "l2")
         l3 = load_list(offs3, "l3")
         ws_w = load_words(nc.sync, ws_words[0].rearrange("p c r -> p (c r)"), 4 * N, "ws_w")
@@ -115,15 +115,15 @@ def tile_list_postedtwice_solo_further_tabled_kernel(
 
         x5_w, x5_s = gather_tokens(l5, "x5", "w_s")
         H = O // 2
-        p_ps = []
+        p_ps = {}
         for h in range(2):
-            acc = psum.tile([P, N // P, H], F32, name="p_ps%d" % h)
             reads = slice(h * H, (h + 1) * H)
             for c in range(N // P):
                 cols = slice(c * P, (c + 1) * P)
-                nc.tensor.matmul_mx(acc[:, c, :], lhsT=ws_w[:, cols].bitcast(E5M2), lhsT_scale=ws_s[:, cols],
-                                    rhs=x5_w[:, reads].bitcast(E4M3), rhs_scale=x5_s[:, reads], start=(c == 0), stop=False)
-            p_ps.append(acc)
+                acc = psum.tile([P, H], F32, name="p_ps%d_%d" % (h, c))
+                p_ps[h, c] = acc
+                nc.tensor.matmul_mx(acc[:], lhsT=ws_w[:, cols].bitcast(E5M2), lhsT_scale=ws_s[:, cols],
+                                    rhs=x5_w[:, reads].bitcast(E4M3), rhs_scale=x5_s[:, reads], start=True, stop=False)
 
         a_sb = [sb([P, J], F32, "a_sb%d" % t) for t in range(PACK)]
         boards = []
@@ -177,11 +177,10 @@ def tile_list_postedtwice_solo_further_tabled_kernel(
             nc.vector.quantize_mx(hid_w[h][:].bitcast(E4M3), hid_s[h][:], hid[h][:].rearrange("p o t -> p (o t)"))
             for c in range(N // P):
                 cols = slice(c * P, (c + 1) * P)
-                nc.tensor.matmul_mx(p_ps[h][:, c, :], lhsT=wb_w[:, cols].bitcast(E5M2), lhsT_scale=wb_s[:, cols],
-                                    rhs=hid_w[h][:].bitcast(E4M3), rhs_scale=hid_s[h][:], start=False, stop=(c == N // P - 1))
-        out_rows = out.rearrange("(c p) o -> p c o", p=P)
+                nc.tensor.matmul_mx(p_ps[h, c][:], lhsT=wb_w[:, cols].bitcast(E5M2), lhsT_scale=wb_s[:, cols],
+                                    rhs=hid_w[h][:].bitcast(E4M3), rhs_scale=hid_s[h][:], start=False, stop=True)
         for h in range(2):
-            reads = slice(h * H, (h + 1) * H)
-            y = sb([P, N // P, H], F32, "y%d" % h)
-            nc.vector.tensor_tensor(y[:], p_ps[h][:], tzg[:, h], ALU.add)
-            nc.sync.dma_start(out_rows[:, :, reads], y[:])
+            for c in range(N // P):
+                y = sb([P, H], F32, "y%d_%d" % (h, c))
+                nc.vector.tensor_tensor(y[:], p_ps[h, c][:], tzg[:, h, c, :], ALU.add)
+                nc.sync.dma_start(out[c * P : (c + 1) * P, h * H : (h + 1) * H], y[:])

from contextlib import ExitStack

import concourse.mybir as mybir

K, T, J, R, C, O, N, E = 512, 1024, 256, 512, 512, 256, 256, 1024
FLOPS = 2 * K * R * J + 2 * R * N * O + 2 * K * N * O

F32 = mybir.dt.float32
BF16 = mybir.dt.bfloat16
I32 = mybir.dt.int32
U32 = mybir.dt.uint32
U16 = mybir.dt.uint16
U8 = mybir.dt.uint8
E4M3 = mybir.dt.float8_e4m3fn_x4
E5M2 = mybir.dt.float8_e5m2_x4
E2M1 = mybir.dt.float4_e2m1fn_x4
ALU = mybir.AluOpType
COPY = mybir.ActivationFunctionType.Copy

P = 128
PACK = 4


def tile_list_postedtwice_solo_further_tabled_kernel(
    tc, xt_words, xt_scales, w_words, w_scales, wb_words, wb_scales, ws_words, ws_scales, tz,
    offs, offs2, offs3, offs4, offs5, offs6, out,
):
    nc = tc.nc
    with ExitStack() as ctx:
        keep = ctx.enter_context(tc.tile_pool(name="keep", bufs=1))
        psum = ctx.enter_context(tc.psum_pool(name="psum", bufs=1))

        def sb(shape, dtype, name):
            return keep.tile(shape, dtype, name=name, align_bytes=64)

        def load_list(src, name):
            t = sb([P, 16], U16, name)
            nc.sync.dma_start(t[:], src)
            return t

        def load_words(queue, src2d, width_bytes, name):
            t = sb([P, width_bytes // 4], I32, name)
            queue.dma_start(t[:], src2d.bitcast(I32))
            return t

        def load_scale_rows(plane, src, q, queue=nc.sync):
            queue.dma_start(plane[32 * q : 32 * q + 4, :].bitcast(I32), src[0, 4 * q : 4 * q + 4, :].bitcast(I32))

        def load_token_scales(queue, q):
            rows = xt_scales[0, 4 * q : 4 * q + 4, :].bitcast(I32)
            queue.dma_start(xt_s[32 * q : 32 * (q + 1), :].bitcast(I32), rows.unsqueeze(0).to_broadcast([8, 4, T // 4]))

        xt_s = sb([P, T], U8, "xt_s")
        w_s = keep.tile([P, R], U8, name="w_s", tag="w_s", align_bytes=64)
        ws_s = sb([P, N], U8, "ws_s")
        wb_s = sb([P, N], U8, "wb_s")
        for plane in (w_s, ws_s, wb_s):
            nc.gpsimd.memset(plane[:].bitcast(I32), 0)

        l1 = load_list(offs, "l1")
        l5 = load_list(offs5, "l5")
        for q in range(3):
            load_token_scales(nc.scalar, q)
        load_token_scales(nc.sync, 3)
        xt_w = load_words(nc.sync, xt_words[0].rearrange("p c r -> p (c r)"), 4 * T, "xt_w")
        w_w = load_words(nc.scalar, w_words[0], 2 * R, "w_w")
        for q in range(4):
            load_scale_rows(w_s, w_scales, q, nc.sync if q % 2 == 0 else nc.scalar)
        l2 = load_list(offs2, "l2")
        l3 = load_list(offs3, "l3")
        ws_w = load_words(nc.sync, ws_words[0].rearrange("p c r -> p (c r)"), 4 * N, "ws_w")
        wb_w = load_words(nc.sync, wb_words[0].rearrange("p c r -> p (c r)"), 4 * N, "wb_w")
        for q in range(4):
            load_scale_rows(ws_s, ws_scales, q)
        l4 = load_list(offs4, "l4")
        for q in range(4):
            load_scale_rows(wb_s, wb_scales, q)
        l6 = load_list(offs6, "l6")
        tz_t = []
        for c in range(N // P):
            t = sb([P, E], F32, "tz%d" % c)
            nc.sync.dma_start(t[:], tz[c * P : (c + 1) * P, :])
            tz_t.append(t)

        BOARDS = 3
        pw = [sb([P, C], F32, "pw%d" % t) for t in range(BOARDS)]
        pv = [sb([P, C], F32, "pv%d" % t) for t in range(BOARDS)]
        for t in range(BOARDS):
            nc.vector.memset(pw[t][:], 0.0)
            nc.vector.memset(pv[t][:], 0.0)

        def gather_tokens(lst, name, words_tag):
            gs = sb([P, J], U8, name + "_s")
            nc.vector.tensor_copy(gs[:], xt_s[:].indirect(lst[:]))
            gw = keep.tile([P, J], U32, name=name + "_w", tag=words_tag, align_bytes=64)
            nc.vector.tensor_copy(gw[:], xt_w[:].bitcast(U32).indirect(lst[:]))
            return gw, gs

        x1_w, x1_s = gather_tokens(l1, "x1", "x1_w")

        a_ps = []
        wt_s0 = sb([P, P], U8, "wt_s0")
        wt_s1 = sb([P, PACK - 1, P], U8, "wt_s1")
        dealt = w_s[:].rearrange("p (m t) -> p t m", t=PACK)
        nc.vector.tensor_copy(wt_s0[:], dealt[:, 0, :])
        nc.vector.tensor_copy(wt_s1[:], dealt[:, 1:, :])
        for t in range(PACK):
            wt_w = sb([P, 2 * P], U8, "wt_w%d" % t)
            nc.scalar.copy(wt_w[:].bitcast(U16), w_w[:].bitcast(U16)[:, t : R : PACK])
            wt_s = wt_s0[:] if t == 0 else wt_s1[:, t - 1, :]
            acc = psum.tile([P, J], F32, name="a_ps%d" % t)
            nc.tensor.matmul_mx(acc[:], lhsT=wt_w[:].bitcast(E2M1), lhsT_scale=wt_s,
                                rhs=x1_w[:].bitcast(E4M3), rhs_scale=x1_s[:], start=True, stop=True)
            a_ps.append(acc)

        x5_w, x5_s = gather_tokens(l5, "x5", "w_s")
        H = O // 2
        p_ps = {}
        for h in range(2):
            reads = slice(h * H, (h + 1) * H)
            for c in range(N // P):
                cols = slice(c * P, (c + 1) * P)
                acc = psum.tile([P, H], F32, name="p_ps%d_%d" % (h, c))
                p_ps[h, c] = acc
                nc.tensor.matmul_mx(acc[:], lhsT=ws_w[:, cols].bitcast(E5M2), lhsT_scale=ws_s[:, cols],
                                    rhs=x5_w[:, reads].bitcast(E4M3), rhs_scale=x5_s[:, reads], start=True, stop=False)

        a_sb = [sb([P, J], F32, "a_sb%d" % t) for t in range(PACK)]
        boards = []
        picked = sb([P, PACK, O], F32, "picked")

        def post(t):
            nc.vector.tensor_copy(pw[t % BOARDS][:].indirect(l2[:]), a_sb[t][:])
            nc.scalar.activation(pv[t % BOARDS][:].indirect(l3[:]), a_sb[t][:], COPY)

        def add(t):
            board = keep.tile([P, C], F32, name="pg%d" % t, tag="pg%d" % (t % BOARDS), align_bytes=64)
            (nc.gpsimd if t < PACK - 1 else nc.vector).tensor_tensor(board[:], pw[t % BOARDS][:], pv[t % BOARDS][:], ALU.add)
            return board

        def read(t, board):
            if t == 0:
                nc.vector.tensor_copy(picked[:, t, :], board[:].indirect(l4[:]))
            elif t < PACK - 1:
                nc.scalar.activation(picked[:, t, :], board[:].indirect(l4[:]), COPY)
            else:
                nc.scalar.activation(picked[:, t, :H], board[:].indirect(l4[:, : H // 16]), COPY)
                nc.scalar.activation(picked[:, t, H:], board[:].indirect(l4[:, H // 16 :]), COPY)

        nc.scalar.copy(a_sb[0][:], a_ps[0][:])
        for t in range(PACK):
            post(t)
            if t == 0:
                nc.vector.tensor_copy(a_sb[1][:], a_ps[1][:])
            if t + 2 < PACK:
                nc.scalar.copy(a_sb[t + 2][:], a_ps[t + 2][:])
            if t < PACK - 1:
                boards.append(add(t))
        read(0, boards[0])
        boards.append(add(PACK - 1))
        for t in range(1, PACK):
            read(t, boards[t])

        tzg = keep.tile([P, 2, N // P, H], F32, name="tzg", tag="pg0", align_bytes=64)
        for h in range(2):
            for c in range(N // P):
                nc.scalar.activation(tzg[:, h, c, :], tz_t[c][:].indirect(l6[:, h * H // 16 : (h + 1) * H // 16]), COPY)

        hid, hid_w, hid_s = [], [], []
        for h in range(2):
            hid.append(sb([P, H, PACK], BF16, "hid%d" % h))
            nc.vector.tensor_scalar_max(hid[h][:].rearrange("p (g i) t -> p g t i", i=4),
                                        picked[:, :, h * H : (h + 1) * H].rearrange("p t (g i) -> p g t i", i=4), 0.0)
        for h in range(2):
            hid_w.append(sb([P, H], U32, "hid_w%d" % h))
            hid_s.append(sb([P, H], U8, "hid_s%d" % h))
            nc.vector.quantize_mx(hid_w[h][:].bitcast(E4M3), hid_s[h][:], hid[h][:].rearrange("p o t -> p (o t)"))
            for c in range(N // P):
                cols = slice(c * P, (c + 1) * P)
                nc.tensor.matmul_mx(p_ps[h, c][:], lhsT=wb_w[:, cols].bitcast(E5M2), lhsT_scale=wb_s[:, cols],
                                    rhs=hid_w[h][:].bitcast(E4M3), rhs_scale=hid_s[h][:], start=False, stop=True)
        for h in range(2):
            for c in range(N // P):
                y = sb([P, H], F32, "y%d_%d" % (h, c))
                nc.vector.tensor_tensor(y[:], p_ps[h, c][:], tzg[:, h, c, :], ALU.add)
                nc.sync.dma_start(out[c * P : (c + 1) * P, h * H : (h + 1) * H], y[:])
